import numpy as np
import ml_dtypes


def mxq(x, axis, fmt="e4m3"):
    dtype, down = {"e4m3": (ml_dtypes.float8_e4m3fn, 7), "e5m2": (ml_dtypes.float8_e5m2, 14)}[fmt]
    v = np.moveaxis(np.asarray(x, np.float32).astype(ml_dtypes.bfloat16).astype(np.float64), axis, -1)
    blocks = v.reshape(v.shape[:-1] + (-1, 32))
    amax = np.abs(blocks).max(-1, keepdims=True)
    byte = np.maximum(np.where(amax > 0, np.frexp(amax)[1] - 1 + 127, 0) - down, 1)
    scale = np.exp2(byte - 127.0)
    codes = (blocks / scale).astype(np.float32).astype(dtype).astype(np.float64)
    return np.moveaxis((codes * scale).reshape(v.shape), -1, axis)


WIDE = False


def mx_kscale(k):
    if not WIDE:
        return np.ones(k)
    levels = np.array([10, -10, 5, -5, 0])
    if k % 512:
        return np.exp2(np.random.permutation(np.resize(levels, k // 32))).repeat(32)
    a = np.empty((k // 512, 16))
    for p in range(k // 512):
        a[p, :8] = np.random.permutation(np.resize(levels, 8))
        for g in range(8):
            far = levels[np.abs(levels - a[p, g]) >= 10]
            a[p, g + 8] = far[np.random.randint(len(far))]
    return np.exp2(a.ravel()).repeat(32)


def f64(x):
    return np.asarray(x).astype(np.float64)


def striped(idx):
    return np.tile(idx.reshape(-1, 16).T, (8, 1)).astype(np.uint16)


def unstriped(offs):
    return offs[:16].T.reshape(-1).astype(np.int64)


def striped8(idx):
    return np.concatenate([x.reshape(-1, 16).T for x in idx]).astype(np.uint16)


def runs(offs, k):
    lists = np.stack([offs[16 * r : 16 * r + 16].T.reshape(-1) for r in range(8)]).astype(np.int64)
    return lists[np.arange(k) % 512 // 64]


def pack_weight(w):
    k, n = w.shape
    w = f64(np.asarray(w, np.float32).astype(ml_dtypes.bfloat16)).reshape(k // 32, 32, n)
    amax = np.abs(w).max(1)
    byte = np.clip(np.where(amax > 0, np.frexp(amax)[1] - 1 + 127 - 7, 1), 1, 254)
    scaled = (w * np.exp2(127.0 - byte)[:, None, :]).reshape(k, n).astype(np.float32)
    words = np.ascontiguousarray(scaled.reshape(k // 512, 128, 4, n).transpose(0, 1, 3, 2)).astype(ml_dtypes.float8_e4m3fn).view(np.uint8)
    return words, np.ascontiguousarray(byte.astype(np.uint8).reshape(k // 512, 16, n))


def unpack_weight(words, scales):
    g, p, n, _ = words.shape
    vals = np.ascontiguousarray(words).view(ml_dtypes.float8_e4m3fn).astype(np.float64) * np.repeat(np.exp2(scales.astype(np.float64) - 127.0), 8, axis=1)[..., None]
    return vals.transpose(0, 1, 3, 2).reshape(g * 512, n)


K, T, S, N, G, H, W = 512, 1024, 512, 512, 2048, 512, 256


def setup_inputs():
    n = np.random.standard_normal
    s = mx_kscale(K)[:, None]
    u = mx_kscale(S)
    packed_xT = pack_weight(n((K, T)) * s)
    packed_dT = pack_weight(n((K, G)) / s)
    perm = np.stack([np.random.permutation(S) for _ in range(8)])
    return {
        "x_words": packed_xT[0],
        "x_scales": packed_xT[1],
        "d_words": packed_dT[0],
        "d_scales": packed_dT[1],
        "gn": (np.random.uniform(0.5, 1.5, (H, 1)) * u[:, None]).astype(np.float32),
        "w1": (n((H, N)) / np.sqrt(H) / u[:, None]).astype(np.float32),
        "offs": striped(np.random.permutation(T)[:S]),
        "ka": striped8(np.random.randint(0, G, (8, H))),
        "kb": striped8(np.random.randint(0, G, (8, H))),
        "n1": striped8(perm[:, :W]),
        "n2": striped8(perm[:, W:]),
    }


def reference(x_words, x_scales, d_words, d_scales, gn, w1, offs, ka, kb, n1, n2):
    d_ka = unpack_weight(d_words, d_scales)[np.arange(K)[:, None], runs(ka, K)]
    xq = unpack_weight(x_words, x_scales)[:, unstriped(offs)]
    d_kb = unpack_weight(d_words, d_scales)[np.arange(K)[:, None], runs(kb, K)]
    h = 0.0625 * (d_ka.T @ xq + d_kb.T @ xq)
    z = f64(gn) * h
    h2 = mxq(f64(w1), 0, "e4m3").T @ mxq(z, 0, "e4m3")
    pa = h2[np.arange(N)[:, None], runs(n1, N)]
    pb = h2[np.arange(N)[:, None], runs(n2, N)]
    ra = np.maximum(pa, pb)
    out = h2.copy()
    out[np.arange(N)[:, None], runs(n1, N)] = ra
    return out

@@ -1,0 +1,188 @@
+from contextlib import ExitStack
+
+import concourse.mybir as mybir
+
+F32 = mybir.dt.float32
+BF16 = mybir.dt.bfloat16
+I32 = mybir.dt.int32
+U32 = mybir.dt.uint32
+U16 = mybir.dt.uint16
+U8 = mybir.dt.uint8
+FP8X4 = mybir.dt.float8_e4m3fn_x4
+MULT = mybir.AluOpType.mult
+COPY = mybir.ActivationFunctionType.Copy
+
+P = 128
+PACK = 4
+K, T, S, N, G, H, W = 512, 1024, 512, 512, 2048, 512, 256
+CHUNK = 128
+CHUNKS = S // CHUNK
+
+FLOPS = 2 * (2 * K * H * S + H * N * S)
+
+
+def tile_picked_aqlifill_none_p_kernel(
+    tc, x_words, x_scales, d_words, d_scales, gn, w1, offs, ka, kb, n1, n2, out
+):
+    nc = tc.nc
+    with ExitStack() as ctx:
+        keep = ctx.enter_context(tc.tile_pool(name="keep", bufs=1))
+        psum = ctx.enter_context(tc.psum_pool(name="psum", bufs=1))
+
+        def sb(name, width, dtype, tag=None):
+            return keep.tile([P, width], dtype, name=name, tag=tag or name, align_bytes=64)
+
+        ka_list = sb("ka_list", H // 16, U16)
+        kb_list = sb("kb_list", H // 16, U16)
+        offs_list = sb("offs_list", S // 16, U16)
+        n1_list = sb("n1_list", W // 16, U16)
+        n2_list = sb("n2_list", W // 16, U16)
+
+        d_table = sb("d_table", G, U32)
+        x_table = sb("x_table", T, U32)
+        d_scale_table = sb("d_scale_table", G, U8)
+        x_scale_table = sb("x_scale_table", T, U8)
+
+        nc.sync.dma_start(offs_list[:], offs)
+        nc.sync.dma_start(x_scale_table[:].bitcast(I32), x_scales[0].bitcast(I32).unsqueeze(1).to_broadcast([16, 8, T // 4]))
+        nc.sync.dma_start(ka_list[:], ka)
+        nc.sync.dma_start(d_scale_table[:].bitcast(I32), d_scales[0].bitcast(I32).unsqueeze(1).to_broadcast([16, 8, G // 4]))
+        nc.sync.dma_start(kb_list[:], kb)
+
+        w_raw = keep.tile([P, PACK, N], F32, name="w_raw", align_bytes=64)
+        w_rows = w1.rearrange("(g t r) m -> t g r m", t=PACK, r=8)
+        for t in range(PACK):
+            nc.sync.dma_start(w_raw[:, t, :], w_rows[t])
+        nc.sync.dma_start(x_table[:].bitcast(I32), x_words[0].rearrange("p n t -> p (n t)").bitcast(I32))
+        nc.sync.dma_start(d_table[:].bitcast(I32), d_words[0].rearrange("p n t -> p (n t)").bitcast(I32))
+        gain_raw = keep.tile([P, PACK, 8], F32, name="gain_raw", align_bytes=64)
+        gn_rows = gn.rearrange("(g t r) o -> t g (r o)", t=PACK, r=8)
+        with nc.allow_non_contiguous_dma(reason="one gain a partition"):
+            for t in range(PACK):
+                nc.sync.dma_start(gain_raw[:, t, 0:1], gn_rows[t])
+        nc.sync.dma_start(n2_list[:], n2)
+        nc.sync.dma_start(n1_list[:], n1)
+        gain = sb("gain", PACK, F32)
+        nc.scalar.activation(gain[:], gain_raw[:, :, 0], COPY, scale=0.0625)
+
+        d_bytes = sb("d_bytes", 2 * H, U8)
+        x_bytes = sb("x_bytes", S, U8)
+        nc.vector.tensor_copy(x_bytes[:], x_scale_table[:].indirect(offs_list[:]))
+        nc.vector.tensor_copy(d_bytes[:, 0:H], d_scale_table[:].indirect(ka_list[:]))
+        nc.vector.tensor_copy(d_bytes[:, H : 2 * H], d_scale_table[:].indirect(kb_list[:]))
+        planes = sb("planes", 2 * H + S, U8)
+        nc.vector.tensor_copy(
+            planes[:, 0 : 2 * H].bitcast(I32).rearrange("p (l t g w) -> p l t g w", l=2, t=PACK, w=2),
+            d_bytes[:].bitcast(I32).rearrange("p (l g t w) -> p l t g w", l=2, t=PACK, w=2),
+        )
+        nc.vector.tensor_copy(planes[:, 2 * H :].bitcast(I32), x_bytes[:].bitcast(I32))
+        for e in range(1, 4):
+            nc.sync.dma_start(planes[e:P:32, :].bitcast(I32), planes[8 * e : P : 32, :].bitcast(I32))
+
+        x_first = sb("x_first", S // 2, U32)
+        nc.vector.tensor_copy(x_first[:], x_table[:].indirect(offs_list[:, 0 : S // 32]))
+        d_codes = []
+        for name, picks in (("a", ka_list), ("b", kb_list)):
+            picked = sb("picked_" + name, H, U32)
+            dealt = sb("dealt_" + name, H, U32)
+            nc.vector.tensor_copy(picked[:], d_table[:].indirect(picks[:]))
+            nc.vector.tensor_copy(
+                dealt[:].rearrange("p (t g r) -> p t g r", t=PACK, r=8),
+                picked[:].rearrange("p (g t r) -> p t g r", t=PACK, r=8),
+            )
+            d_codes.append(dealt)
+        x_second = sb("x_second", S // 2, U32, tag="picked_a")
+        nc.vector.tensor_copy(x_second[:], x_table[:].indirect(offs_list[:, S // 32 : S // 16]))
+        x_codes = [x_first, x_second]
+
+        w_bf = sb("w_bf", PACK * N, BF16)
+        nc.scalar.copy(
+            w_bf[:].rearrange("p (u m j) -> p m u j", u=PACK, j=PACK),
+            w_raw[:].rearrange("p j (m u) -> p m u j", u=PACK),
+        )
+        w_codes = sb("w_codes", N, U32, tag="picked_b")
+        w_plane = sb("w_plane", N, U8)
+        nc.vector.quantize_mx(out=w_codes[:].bitcast(FP8X4), scales=w_plane[:], in_=w_bf[:])
+
+        h_banks = [psum.tile([P, PACK * CHUNK], F32, name="h_bank%d" % c) for c in range(CHUNKS)]
+        h2_banks = [psum.tile([P, PACK * CHUNK], F32, name="h2_bank%d" % c) for c in range(CHUNKS - 1)]
+
+        def first_product(c, half):
+            cols = slice(c % 2 * CHUNK, (c % 2 + 1) * CHUNK)
+            scale_cols = slice(2 * H + c * CHUNK, 2 * H + (c + 1) * CHUNK)
+            for t in range(PACK):
+                nc.tensor.matmul_mx(
+                    out=h_banks[c][:, t * CHUNK : (t + 1) * CHUNK],
+                    lhsT=d_codes[half][:, t * P : (t + 1) * P].bitcast(FP8X4),
+                    lhsT_scale=planes[:, half * H + t * P : half * H + (t + 1) * P],
+                    rhs=x_codes[c // 2][:, cols].bitcast(FP8X4),
+                    rhs_scale=planes[:, scale_cols],
+                    start=(half == 0 and t == 0),
+                    stop=(half == 1 and t == PACK - 1),
+                )
+
+        for c in range(CHUNKS):
+            first_product(c, 0)
+            first_product(c, 1)
+
+        rows = [sb("rows%d" % u, S, F32) for u in range(PACK)]
+        z_bf = [sb("z_bf%d" % c, PACK * CHUNK, BF16) for c in range(CHUNKS)]
+
+        def scale_and_round(c):
+            nc.vector.tensor_tensor(
+                out=z_bf[c][:].rearrange("p (n t) -> p n t", t=PACK),
+                in0=h_banks[c][:].rearrange("p (t n) -> p n t", t=PACK),
+                in1=gain[:].unsqueeze(1).to_broadcast([P, CHUNK, PACK]),
+                op=MULT,
+            )
+
+        def h2_place(c, u):
+            if c == CHUNKS - 1:
+                return h_banks[u][:, 0:CHUNK]
+            return h2_banks[c][:, u * CHUNK : (u + 1) * CHUNK]
+
+        def leave_psum(c, u):
+            nc.scalar.copy(rows[u][:, c * CHUNK : (c + 1) * CHUNK], h2_place(c, u))
+
+        def second_product(c):
+            z_codes = sb("z_codes%d" % c, CHUNK, U32)
+            z_plane = sb("z_plane%d" % c, CHUNK, U8)
+            nc.vector.quantize_mx(out=z_codes[:].bitcast(FP8X4), scales=z_plane[:], in_=z_bf[c][:])
+            for u in range(PACK):
+                nc.tensor.matmul_mx(
+                    out=h2_place(c, u),
+                    lhsT=w_codes[:, u * P : (u + 1) * P].bitcast(FP8X4),
+                    lhsT_scale=w_plane[:, u * P : (u + 1) * P],
+                    rhs=z_codes[:].bitcast(FP8X4),
+                    rhs_scale=z_plane[:],
+                    start=True,
+                    stop=True,
+                )
+
+        scale_and_round(0)
+        for c in range(CHUNKS):
+            if c + 1 < CHUNKS:
+                scale_and_round(c + 1)
+            second_product(c)
+            if c + 1 < CHUNKS:
+                for u in range(PACK):
+                    leave_psum(c, u)
+
+        out_rows = out.rearrange("(p u) j -> u p j", u=PACK)
+        pa = sb("pa", PACK * W, F32)
+        pb = sb("pb", PACK * W, F32)
+        ra = sb("ra", PACK * W, F32)
+        for group in ((0,), (1,), (2, 3)):
+            for u in group:
+                mine = slice(u * W, (u + 1) * W)
+                leave_psum(CHUNKS - 1, u)
+                nc.scalar.activation(pb[:, mine], rows[u][:].indirect(n2_list[:]), COPY)
+                if u == 0:
+                    nc.vector.tensor_copy(pa[:, mine], rows[u][:].indirect(n1_list[:]))
+                else:
+                    nc.scalar.activation(pa[:, mine], rows[u][:].indirect(n1_list[:]), COPY)
+            both = slice(group[0] * W, (group[-1] + 1) * W)
+            nc.vector.tensor_max(ra[:, both], pa[:, both], pb[:, both])
+            for u in group:
+                nc.vector.tensor_copy(rows[u][:].indirect(n1_list[:]), ra[:, u * W : (u + 1) * W])
+                nc.sync.dma_start(out_rows[u], rows[u][:])

@@ -17,6 +17,8 @@ PACK = 4
 K, T, S, N, G, H, W = 512, 1024, 512, 512, 2048, 512, 256
 CHUNK = 128
 CHUNKS = S // CHUNK
+HALF = S // 2
+EARLY = 384
 
 FLOPS = 2 * (2 * K * H * S + H * N * S)
 
@@ -49,21 +51,15 @@ def tile_picked_aqlifill_none_p_kernel(
         nc.sync.dma_start(d_scale_table[:].bitcast(I32), d_scales[0].bitcast(I32).unsqueeze(1).to_broadcast([16, 8, G // 4]))
         nc.sync.dma_start(kb_list[:], kb)
 
-        w_raw = keep.tile([P, PACK, N], F32, name="w_raw", align_bytes=64)
-        w_rows = w1.rearrange("(g t r) m -> t g r m", t=PACK, r=8)
-        for t in range(PACK):
-            nc.sync.dma_start(w_raw[:, t, :], w_rows[t])
         nc.sync.dma_start(x_table[:].bitcast(I32), x_words[0].rearrange("p n t -> p (n t)").bitcast(I32))
         nc.sync.dma_start(d_table[:].bitcast(I32), d_words[0].rearrange("p n t -> p (n t)").bitcast(I32))
-        gain_raw = keep.tile([P, PACK, 8], F32, name="gain_raw", align_bytes=64)
-        gn_rows = gn.rearrange("(g t r) o -> t g (r o)", t=PACK, r=8)
-        with nc.allow_non_contiguous_dma(reason="one gain a partition"):
-            for t in range(PACK):
-                nc.sync.dma_start(gain_raw[:, t, 0:1], gn_rows[t])
+        gain = sb("gain", PACK, F32)
+        nc.sync.dma_start(gain[:], gn.rearrange("(p t) o -> p (t o)", t=PACK))
+        w_rows = w1.rearrange("(p t) m -> p t m", t=PACK)
+        w_first = keep.tile([P, PACK, EARLY], F32, name="w_first", align_bytes=64)
+        nc.sync.dma_start(w_first[:], w_rows[:, :, 0:EARLY])
         nc.sync.dma_start(n2_list[:], n2)
         nc.sync.dma_start(n1_list[:], n1)
-        gain = sb("gain", PACK, F32)
-        nc.scalar.activation(gain[:], gain_raw[:, :, 0], COPY, scale=0.0625)
 
         d_bytes = sb("d_bytes", 2 * H, U8)
         x_bytes = sb("x_bytes", S, U8)
@@ -72,12 +68,14 @@ def tile_picked_aqlifill_none_p_kernel(
         nc.vector.tensor_copy(d_bytes[:, H : 2 * H], d_scale_table[:].indirect(kb_list[:]))
         planes = sb("planes", 2 * H + S, U8)
         nc.vector.tensor_copy(
-            planes[:, 0 : 2 * H].bitcast(I32).rearrange("p (l t g w) -> p l t g w", l=2, t=PACK, w=2),
-            d_bytes[:].bitcast(I32).rearrange("p (l g t w) -> p l t g w", l=2, t=PACK, w=2),
+            planes[:, 0 : 2 * H].rearrange("p (l t a b) -> p l a t b", l=2, t=PACK, b=16),
+            d_bytes[:].rearrange("p (l a b t) -> p l a t b", l=2, t=PACK, b=16),
         )
         nc.vector.tensor_copy(planes[:, 2 * H :].bitcast(I32), x_bytes[:].bitcast(I32))
         for e in range(1, 4):
             nc.sync.dma_start(planes[e:P:32, :].bitcast(I32), planes[8 * e : P : 32, :].bitcast(I32))
+        w_second = keep.tile([P, PACK, N - EARLY], F32, name="w_second", tag="d_bytes", align_bytes=64)
+        nc.sync.dma_start(w_second[:], w_rows[:, :, EARLY:N])
 
         x_first = sb("x_first", S // 2, U32)
         nc.vector.tensor_copy(x_first[:], x_table[:].indirect(offs_list[:, 0 : S // 32]))
@@ -87,8 +85,8 @@ def tile_picked_aqlifill_none_p_kernel(
             dealt = sb("dealt_" + name, H, U32)
             nc.vector.tensor_copy(picked[:], d_table[:].indirect(picks[:]))
             nc.vector.tensor_copy(
-                dealt[:].rearrange("p (t g r) -> p t g r", t=PACK, r=8),
-                picked[:].rearrange("p (g t r) -> p t g r", t=PACK, r=8),
+                dealt[:].rearrange("p (t a b) -> p a t b", t=PACK, b=4),
+                picked[:].rearrange("p (a b t) -> p a t b", t=PACK, b=4),
             )
             d_codes.append(dealt)
         x_second = sb("x_second", S // 2, U32, tag="picked_a")
@@ -96,16 +94,15 @@ def tile_picked_aqlifill_none_p_kernel(
         x_codes = [x_first, x_second]
 
         w_bf = sb("w_bf", PACK * N, BF16)
-        nc.scalar.copy(
-            w_bf[:].rearrange("p (u m j) -> p m u j", u=PACK, j=PACK),
-            w_raw[:].rearrange("p j (m u) -> p m u j", u=PACK),
-        )
+        w_slots = w_bf[:].rearrange("p (u m j) -> p m u j", u=PACK, j=PACK)
+        nc.scalar.copy(w_slots[:, 0 : EARLY // PACK], w_first[:].rearrange("p j (m u) -> p m u j", u=PACK))
+        nc.scalar.copy(w_slots[:, EARLY // PACK : P], w_second[:].rearrange("p j (m u) -> p m u j", u=PACK))
         w_codes = sb("w_codes", N, U32, tag="picked_b")
         w_plane = sb("w_plane", N, U8)
         nc.vector.quantize_mx(out=w_codes[:].bitcast(FP8X4), scales=w_plane[:], in_=w_bf[:])
 
         h_banks = [psum.tile([P, PACK * CHUNK], F32, name="h_bank%d" % c) for c in range(CHUNKS)]
-        h2_banks = [psum.tile([P, PACK * CHUNK], F32, name="h2_bank%d" % c) for c in range(CHUNKS - 1)]
+        h2_banks = [psum.tile([P, 2 * HALF], F32, name="h2_bank%d" % b) for b in range(2)]
 
         def first_product(c, half):
             cols = slice(c % 2 * CHUNK, (c % 2 + 1) * CHUNK)
@@ -126,31 +123,34 @@ def tile_picked_aqlifill_none_p_kernel(
             first_product(c, 1)
 
         rows = [sb("rows%d" % u, S, F32) for u in range(PACK)]
-        z_bf = [sb("z_bf%d" % c, PACK * CHUNK, BF16) for c in range(CHUNKS)]
+        z_bf = [sb("z_bf%d" % half, PACK * HALF, BF16) for half in range(2)]
 
         def scale_and_round(c):
-            nc.vector.tensor_tensor(
-                out=z_bf[c][:].rearrange("p (n t) -> p n t", t=PACK),
+            cols = slice(c % 2 * PACK * CHUNK, (c % 2 + 1) * PACK * CHUNK)
+            nc.vector.scalar_tensor_tensor(
+                out=z_bf[c // 2][:, cols].rearrange("p (n t) -> p n t", t=PACK),
                 in0=h_banks[c][:].rearrange("p (t n) -> p n t", t=PACK),
+                scalar=0.0625,
                 in1=gain[:].unsqueeze(1).to_broadcast([P, CHUNK, PACK]),
-                op=MULT,
+                op0=MULT,
+                op1=MULT,
             )
 
-        def h2_place(c, u):
-            if c == CHUNKS - 1:
-                return h_banks[u][:, 0:CHUNK]
-            return h2_banks[c][:, u * CHUNK : (u + 1) * CHUNK]
+        def h2_place(half, u):
+            if half == 1:
+                return h_banks[u][:, 0:HALF]
+            return h2_banks[u // 2][:, u % 2 * HALF : (u % 2 + 1) * HALF]
 
-        def leave_psum(c, u):
-            nc.scalar.copy(rows[u][:, c * CHUNK : (c + 1) * CHUNK], h2_place(c, u))
+        def leave_psum(half, u):
+            nc.scalar.copy(rows[u][:, half * HALF : (half + 1) * HALF], h2_place(half, u))
 
-        def second_product(c):
-            z_codes = sb("z_codes%d" % c, CHUNK, U32)
-            z_plane = sb("z_plane%d" % c, CHUNK, U8)
-            nc.vector.quantize_mx(out=z_codes[:].bitcast(FP8X4), scales=z_plane[:], in_=z_bf[c][:])
+        def second_product(half):
+            z_codes = sb("z_codes%d" % half, HALF, U32)
+            z_plane = sb("z_plane%d" % half, HALF, U8)
+            nc.vector.quantize_mx(out=z_codes[:].bitcast(FP8X4), scales=z_plane[:], in_=z_bf[half][:])
             for u in range(PACK):
                 nc.tensor.matmul_mx(
-                    out=h2_place(c, u),
+                    out=h2_place(half, u),
                     lhsT=w_codes[:, u * P : (u + 1) * P].bitcast(FP8X4),
                     lhsT_scale=w_plane[:, u * P : (u + 1) * P],
                     rhs=z_codes[:].bitcast(FP8X4),
@@ -159,14 +159,13 @@ def tile_picked_aqlifill_none_p_kernel(
                     stop=True,
                 )
 
-        scale_and_round(0)
-        for c in range(CHUNKS):
-            if c + 1 < CHUNKS:
-                scale_and_round(c + 1)
-            second_product(c)
-            if c + 1 < CHUNKS:
-                for u in range(PACK):
-                    leave_psum(c, u)
+        for c in range(3):
+            scale_and_round(c)
+        second_product(0)
+        for u in range(PACK):
+            leave_psum(0, u)
+        scale_and_round(3)
+        second_product(1)
 
         out_rows = out.rearrange("(p u) j -> u p j", u=PACK)
         pa = sb("pa", PACK * W, F32)
@@ -175,7 +174,7 @@ def tile_picked_aqlifill_none_p_kernel(
         for group in ((0,), (1,), (2, 3)):
             for u in group:
                 mine = slice(u * W, (u + 1) * W)
-                leave_psum(CHUNKS - 1, u)
+                leave_psum(1, u)
                 nc.scalar.activation(pb[:, mine], rows[u][:].indirect(n2_list[:]), COPY)
                 if u == 0:
                     nc.vector.tensor_copy(pa[:, mine], rows[u][:].indirect(n1_list[:]))

@@ -29,10 +29,14 @@ def tile_picked_aqlifill_none_p_kernel(
     nc = tc.nc
     with ExitStack() as ctx:
         keep = ctx.enter_context(tc.tile_pool(name="keep", bufs=1))
+        turns = ctx.enter_context(tc.tile_pool(name="turns", bufs=1))
         psum = ctx.enter_context(tc.psum_pool(name="psum", bufs=1))
 
         def sb(name, width, dtype, tag=None):
             return keep.tile([P, width], dtype, name=name, tag=tag or name, align_bytes=64)
+
+        def tenant(name, width, offset):
+            return turns.tile([P, width], U32, name=name, offset=offset, align_bytes=64)
 
         ka_list = sb("ka_list", H // 16, U16)
         kb_list = sb("kb_list", H // 16, U16)
@@ -45,10 +49,10 @@ def tile_picked_aqlifill_none_p_kernel(
         d_scale_table = sb("d_scale_table", G, U8)
         x_scale_table = sb("x_scale_table", T, U8)
 
-        nc.sync.dma_start(offs_list[:], offs)
         nc.sync.dma_start(x_scale_table[:].bitcast(I32), x_scales[0].bitcast(I32).unsqueeze(1).to_broadcast([16, 8, T // 4]))
-        nc.sync.dma_start(ka_list[:], ka)
+        nc.sync.dma_start(offs_list[:], offs)
         nc.sync.dma_start(d_scale_table[:].bitcast(I32), d_scales[0].bitcast(I32).unsqueeze(1).to_broadcast([16, 8, G // 4]))
+        nc.sync.dma_start(ka_list[:], ka)
         nc.sync.dma_start(kb_list[:], kb)
 
         nc.sync.dma_start(x_table[:].bitcast(I32), x_words[0].rearrange("p n t -> p (n t)").bitcast(I32))
@@ -77,32 +81,37 @@ def tile_picked_aqlifill_none_p_kernel(
         w_second = keep.tile([P, PACK, N - EARLY], F32, name="w_second", tag="d_bytes", align_bytes=64)
         nc.sync.dma_start(w_second[:], w_rows[:, :, EARLY:N])
 
-        x_first = sb("x_first", S // 2, U32)
-        nc.vector.tensor_copy(x_first[:], x_table[:].indirect(offs_list[:, 0 : S // 32]))
-        d_codes = []
-        for name, picks in (("a", ka_list), ("b", kb_list)):
-            picked = sb("picked_" + name, H, U32)
-            dealt = sb("dealt_" + name, H, U32)
-            nc.vector.tensor_copy(picked[:], d_table[:].indirect(picks[:]))
+        def deal_words(target, picked):
             nc.vector.tensor_copy(
-                dealt[:].rearrange("p (t a b) -> p a t b", t=PACK, b=4),
+                target[:].rearrange("p (t a b) -> p a t b", t=PACK, b=4),
                 picked[:].rearrange("p (a b t) -> p a t b", t=PACK, b=4),
             )
-            d_codes.append(dealt)
-        x_second = sb("x_second", S // 2, U32, tag="picked_a")
-        nc.vector.tensor_copy(x_second[:], x_table[:].indirect(offs_list[:, S // 32 : S // 16]))
+
+        x_first = sb("x_first", HALF, U32)
+        nc.vector.tensor_copy(x_first[:], x_table[:].indirect(offs_list[:, 0 : HALF // 16]))
+        a_words = tenant("a_words", H, 0)
+        a_codes = sb("a_codes", H, U32)
+        nc.vector.tensor_copy(a_words[:], d_table[:].indirect(ka_list[:]))
+        deal_words(a_codes, a_words)
+        x_second = tenant("x_second", HALF, 0)
+        nc.vector.tensor_copy(x_second[:], x_table[:].indirect(offs_list[:, HALF // 16 : S // 16]))
+        b_words = tenant("b_words", H, 4 * HALF)
+        b_codes = sb("b_codes", H, U32)
+        nc.vector.tensor_copy(b_words[:], d_table[:].indirect(kb_list[:]))
+        deal_words(b_codes, b_words)
         x_codes = [x_first, x_second]
+        d_codes = [a_codes, b_codes]
 
         w_bf = sb("w_bf", PACK * N, BF16)
         w_slots = w_bf[:].rearrange("p (u m j) -> p m u j", u=PACK, j=PACK)
         nc.scalar.copy(w_slots[:, 0 : EARLY // PACK], w_first[:].rearrange("p j (m u) -> p m u j", u=PACK))
         nc.scalar.copy(w_slots[:, EARLY // PACK : P], w_second[:].rearrange("p j (m u) -> p m u j", u=PACK))
-        w_codes = sb("w_codes", N, U32, tag="picked_b")
-        w_plane = sb("w_plane", N, U8)
-        nc.vector.quantize_mx(out=w_codes[:].bitcast(FP8X4), scales=w_plane[:], in_=w_bf[:])
+        w_codes0 = sb("w_codes0", P, U32)
+        w_plane = sb("w_plane", P, U8)
+        nc.vector.quantize_mx(out=w_codes0[:].bitcast(FP8X4), scales=w_plane[:, 0:P], in_=w_bf[:, 0 : PACK * P])
 
         h_banks = [psum.tile([P, PACK * CHUNK], F32, name="h_bank%d" % c) for c in range(CHUNKS)]
-        h2_banks = [psum.tile([P, 2 * HALF], F32, name="h2_bank%d" % b) for b in range(2)]
+        h2_banks = [psum.tile([P, S], F32, name="h2_bank%d" % u) for u in range(PACK)]
 
         def first_product(c, half):
             cols = slice(c % 2 * CHUNK, (c % 2 + 1) * CHUNK)
@@ -120,15 +129,18 @@ def tile_picked_aqlifill_none_p_kernel(
 
         for c in range(CHUNKS):
             first_product(c, 0)
+        for c in (0, 3, 1, 2):
             first_product(c, 1)
 
         rows = [sb("rows%d" % u, S, F32) for u in range(PACK)]
-        z_bf = [sb("z_bf%d" % half, PACK * HALF, BF16) for half in range(2)]
+        z_bf = [sb("z_bf%d" % c, PACK * CHUNK, BF16) for c in range(CHUNKS)]
+        z_codes = sb("z_codes", S, U32)
+        z_plane = sb("z_plane", S, U8)
+        first_banks = [h2_banks[0], h_banks[0], h_banks[1], h_banks[3]]
 
         def scale_and_round(c):
-            cols = slice(c % 2 * PACK * CHUNK, (c % 2 + 1) * PACK * CHUNK)
             nc.vector.scalar_tensor_tensor(
-                out=z_bf[c // 2][:, cols].rearrange("p (n t) -> p n t", t=PACK),
+                out=z_bf[c][:].rearrange("p (n t) -> p n t", t=PACK),
                 in0=h_banks[c][:].rearrange("p (t n) -> p n t", t=PACK),
                 scalar=0.0625,
                 in1=gain[:].unsqueeze(1).to_broadcast([P, CHUNK, PACK]),
@@ -136,52 +148,62 @@ def tile_picked_aqlifill_none_p_kernel(
                 op1=MULT,
             )
 
-        def h2_place(half, u):
-            if half == 1:
-                return h_banks[u][:, 0:HALF]
-            return h2_banks[u // 2][:, u % 2 * HALF : (u % 2 + 1) * HALF]
+        def first_rows(c):
+            cols = slice(c * CHUNK, (c + 1) * CHUNK)
+            nc.vector.quantize_mx(out=z_codes[:, cols].bitcast(FP8X4), scales=z_plane[:, cols], in_=z_bf[c][:])
+            nc.tensor.matmul_mx(
+                out=first_banks[c][:, cols],
+                lhsT=w_codes0[:].bitcast(FP8X4),
+                lhsT_scale=w_plane[:, 0:P],
+                rhs=z_codes[:, cols].bitcast(FP8X4),
+                rhs_scale=z_plane[:, cols],
+                start=True,
+                stop=True,
+            )
+            nc.scalar.copy(rows[0][:, cols], first_banks[c][:, cols])
 
-        def leave_psum(half, u):
-            nc.scalar.copy(rows[u][:, half * HALF : (half + 1) * HALF], h2_place(half, u))
+        gain16 = sb("gain16", PACK, F32)
+        nc.scalar.activation(gain16[:], gain[:], COPY, scale=0.0625)
+        scale_and_round(0)
+        z_flat = sb("z_flat", PACK * CHUNK, BF16)
+        for t in range(PACK):
+            cols = slice(t * CHUNK, (t + 1) * CHUNK)
+            nc.scalar.activation(z_flat[:, cols], h_banks[3][:, cols], COPY, scale=gain16[:, t : t + 1])
+        nc.scalar.copy(
+            z_bf[3][:].rearrange("p (a b t) -> p a t b", t=PACK, b=4),
+            z_flat[:].rearrange("p (t a b) -> p a t b", t=PACK, b=4),
+        )
+        scale_and_round(1)
+        first_rows(0)
+        scale_and_round(2)
+        for c in (1, 3, 2):
+            first_rows(c)
+        w_codes = sb("w_codes", N - P, U32, tag="z_bf2")
+        w_plane_rest = sb("w_plane_rest", N - P, U8)
+        nc.vector.quantize_mx(out=w_codes[:].bitcast(FP8X4), scales=w_plane_rest[:], in_=w_bf[:, PACK * P : PACK * N])
 
-        def second_product(half):
-            z_codes = sb("z_codes%d" % half, HALF, U32)
-            z_plane = sb("z_plane%d" % half, HALF, U8)
-            nc.vector.quantize_mx(out=z_codes[:].bitcast(FP8X4), scales=z_plane[:], in_=z_bf[half][:])
-            for u in range(PACK):
+        out_rows = out.rearrange("(p u) j -> u p j", u=PACK)
+        for u in range(PACK):
+            pa = sb("pa%d" % u, W, F32)
+            pb = sb("pb%d" % u, W, F32)
+            ra = sb("ra%d" % u, W, F32)
+            if u > 0:
+                cols = slice((u - 1) * P, u * P)
                 nc.tensor.matmul_mx(
-                    out=h2_place(half, u),
-                    lhsT=w_codes[:, u * P : (u + 1) * P].bitcast(FP8X4),
-                    lhsT_scale=w_plane[:, u * P : (u + 1) * P],
+                    out=h2_banks[u][:],
+                    lhsT=w_codes[:, cols].bitcast(FP8X4),
+                    lhsT_scale=w_plane_rest[:, cols],
                     rhs=z_codes[:].bitcast(FP8X4),
                     rhs_scale=z_plane[:],
                     start=True,
                     stop=True,
                 )
-
-        for c in range(3):
-            scale_and_round(c)
-        second_product(0)
-        for u in range(PACK):
-            leave_psum(0, u)
-        scale_and_round(3)
-        second_product(1)
-
-        out_rows = out.rearrange("(p u) j -> u p j", u=PACK)
-        pa = sb("pa", PACK * W, F32)
-        pb = sb("pb", PACK * W, F32)
-        ra = sb("ra", PACK * W, F32)
-        for group in ((0,), (1,), (2, 3)):
-            for u in group:
-                mine = slice(u * W, (u + 1) * W)
-                leave_psum(1, u)
-                nc.scalar.activation(pb[:, mine], rows[u][:].indirect(n2_list[:]), COPY)
-                if u == 0:
-                    nc.vector.tensor_copy(pa[:, mine], rows[u][:].indirect(n1_list[:]))
-                else:
-                    nc.scalar.activation(pa[:, mine], rows[u][:].indirect(n1_list[:]), COPY)
-            both = slice(group[0] * W, (group[-1] + 1) * W)
-            nc.vector.tensor_max(ra[:, both], pa[:, both], pb[:, both])
-            for u in group:
-                nc.vector.tensor_copy(rows[u][:].indirect(n1_list[:]), ra[:, u * W : (u + 1) * W])
-                nc.sync.dma_start(out_rows[u], rows[u][:])
+                nc.scalar.copy(rows[u][:], h2_banks[u][:])
+            nc.scalar.activation(pb[:], rows[u][:].indirect(n2_list[:]), COPY)
+            if u == 0:
+                nc.vector.tensor_copy(pa[:], rows[u][:].indirect(n1_list[:]))
+            else:
+                nc.scalar.activation(pa[:], rows[u][:].indirect(n1_list[:]), COPY)
+            nc.vector.tensor_max(ra[:], pa[:], pb[:])
+            nc.vector.tensor_copy(rows[u][:].indirect(n1_list[:]), ra[:])
+            nc.sync.dma_start(out_rows[u], rows[u][:])

from contextlib import ExitStack

import concourse.mybir as mybir

F32 = mybir.dt.float32
BF16 = mybir.dt.bfloat16
I32 = mybir.dt.int32
U32 = mybir.dt.uint32
U16 = mybir.dt.uint16
U8 = mybir.dt.uint8
FP8X4 = mybir.dt.float8_e4m3fn_x4
MULT = mybir.AluOpType.mult
COPY = mybir.ActivationFunctionType.Copy

P = 128
PACK = 4
K, T, S, N, G, H, W = 512, 1024, 512, 512, 2048, 512, 256
CHUNK = 128
CHUNKS = S // CHUNK
HALF = S // 2
EARLY = 384

FLOPS = 2 * (2 * K * H * S + H * N * S)


def tile_picked_aqlifill_none_p_kernel(
    tc, x_words, x_scales, d_words, d_scales, gn, w1, offs, ka, kb, n1, n2, out
):
    nc = tc.nc
    with ExitStack() as ctx:
        keep = ctx.enter_context(tc.tile_pool(name="keep", bufs=1))
        turns = ctx.enter_context(tc.tile_pool(name="turns", bufs=1))
        psum = ctx.enter_context(tc.psum_pool(name="psum", bufs=1))

        def sb(name, width, dtype, tag=None):
            return keep.tile([P, width], dtype, name=name, tag=tag or name, align_bytes=64)

        def tenant(name, width, offset):
            return turns.tile([P, width], U32, name=name, offset=offset, align_bytes=64)

        ka_list = sb("ka_list", H // 16, U16)
        kb_list = sb("kb_list", H // 16, U16)
        offs_list = sb("offs_list", S // 16, U16)
        n1_list = sb("n1_list", W // 16, U16)
        n2_list = sb("n2_list", W // 16, U16)

        d_table = sb("d_table", G, U32)
        x_table = sb("x_table", T, U32)
        d_scale_table = sb("d_scale_table", G, U8)
        x_scale_table = sb("x_scale_table", T, U8)

        nc.sync.dma_start(x_scale_table[:].bitcast(I32), x_scales[0].bitcast(I32).unsqueeze(1).to_broadcast([16, 8, T // 4]))
        nc.sync.dma_start(offs_list[:], offs)
        nc.sync.dma_start(d_scale_table[:].bitcast(I32), d_scales[0].bitcast(I32).unsqueeze(1).to_broadcast([16, 8, G // 4]))
        nc.sync.dma_start(ka_list[:], ka)
        nc.sync.dma_start(kb_list[:], kb)

        nc.sync.dma_start(x_table[:].bitcast(I32), x_words[0].rearrange("p n t -> p (n t)").bitcast(I32))
        nc.sync.dma_start(d_table[:].bitcast(I32), d_words[0].rearrange("p n t -> p (n t)").bitcast(I32))
        gain = sb("gain", PACK, F32)
        nc.sync.dma_start(gain[:], gn.rearrange("(p t) o -> p (t o)", t=PACK))
        w_rows = w1.rearrange("(p t) m -> p t m", t=PACK)
        w_first = keep.tile([P, PACK, EARLY], F32, name="w_first", align_bytes=64)
        nc.sync.dma_start(w_first[:], w_rows[:, :, 0:EARLY])
        nc.sync.dma_start(n2_list[:], n2)
        nc.sync.dma_start(n1_list[:], n1)

        d_bytes = sb("d_bytes", 2 * H, U8)
        x_bytes = sb("x_bytes", S, U8)
        nc.vector.tensor_copy(x_bytes[:], x_scale_table[:].indirect(offs_list[:]))
        nc.vector.tensor_copy(d_bytes[:, 0:H], d_scale_table[:].indirect(ka_list[:]))
        nc.vector.tensor_copy(d_bytes[:, H : 2 * H], d_scale_table[:].indirect(kb_list[:]))
        planes = sb("planes", 2 * H + S, U8)
        nc.vector.tensor_copy(
            planes[:, 0 : 2 * H].rearrange("p (l t a b) -> p l a t b", l=2, t=PACK, b=16),
            d_bytes[:].rearrange("p (l a b t) -> p l a t b", l=2, t=PACK, b=16),
        )
        nc.vector.tensor_copy(planes[:, 2 * H :].bitcast(I32), x_bytes[:].bitcast(I32))
        for e in range(1, 4):
            nc.sync.dma_start(planes[e:P:32, :].bitcast(I32), planes[8 * e : P : 32, :].bitcast(I32))
        w_second = keep.tile([P, PACK, N - EARLY], F32, name="w_second", tag="d_bytes", align_bytes=64)
        nc.sync.dma_start(w_second[:], w_rows[:, :, EARLY:N])

        def deal_words(target, picked):
            nc.vector.tensor_copy(
                target[:].rearrange("p (t a b) -> p a t b", t=PACK, b=4),
                picked[:].rearrange("p (a b t) -> p a t b", t=PACK, b=4),
            )

        x_first = sb("x_first", HALF, U32)
        nc.vector.tensor_copy(x_first[:], x_table[:].indirect(offs_list[:, 0 : HALF // 16]))
        a_words = tenant("a_words", H, 0)
        a_codes = sb("a_codes", H, U32)
        nc.vector.tensor_copy(a_words[:], d_table[:].indirect(ka_list[:]))
        deal_words(a_codes, a_words)
        x_second = tenant("x_second", HALF, 0)
        nc.vector.tensor_copy(x_second[:], x_table[:].indirect(offs_list[:, HALF // 16 : S // 16]))
        b_words = tenant("b_words", H, 4 * HALF)
        b_codes = sb("b_codes", H, U32)
        nc.vector.tensor_copy(b_words[:], d_table[:].indirect(kb_list[:]))
        deal_words(b_codes, b_words)
        x_codes = [x_first, x_second]
        d_codes = [a_codes, b_codes]

        w_bf = sb("w_bf", PACK * N, BF16)
        w_slots = w_bf[:].rearrange("p (u m j) -> p m u j", u=PACK, j=PACK)
        nc.scalar.copy(w_slots[:, 0 : EARLY // PACK], w_first[:].rearrange("p j (m u) -> p m u j", u=PACK))
        nc.scalar.copy(w_slots[:, EARLY // PACK : P], w_second[:].rearrange("p j (m u) -> p m u j", u=PACK))
        w_codes0 = sb("w_codes0", P, U32)
        w_plane = sb("w_plane", P, U8)
        nc.vector.quantize_mx(out=w_codes0[:].bitcast(FP8X4), scales=w_plane[:, 0:P], in_=w_bf[:, 0 : PACK * P])

        h_banks = [psum.tile([P, PACK * CHUNK], F32, name="h_bank%d" % c) for c in range(CHUNKS)]
        h2_banks = [psum.tile([P, S], F32, name="h2_bank%d" % u) for u in range(PACK)]

        def first_product(c, half):
            cols = slice(c % 2 * CHUNK, (c % 2 + 1) * CHUNK)
            scale_cols = slice(2 * H + c * CHUNK, 2 * H + (c + 1) * CHUNK)
            for t in range(PACK):
                nc.tensor.matmul_mx(
                    out=h_banks[c][:, t * CHUNK : (t + 1) * CHUNK],
                    lhsT=d_codes[half][:, t * P : (t + 1) * P].bitcast(FP8X4),
                    lhsT_scale=planes[:, half * H + t * P : half * H + (t + 1) * P],
                    rhs=x_codes[c // 2][:, cols].bitcast(FP8X4),
                    rhs_scale=planes[:, scale_cols],
                    start=(half == 0 and t == 0),
                    stop=(half == 1 and t == PACK - 1),
                )

        for c in range(CHUNKS):
            first_product(c, 0)
        for c in (0, 3, 1, 2):
            first_product(c, 1)

        rows = [sb("rows%d" % u, S, F32) for u in range(PACK)]
        z_bf = [sb("z_bf%d" % c, PACK * CHUNK, BF16) for c in range(CHUNKS)]
        z_codes = sb("z_codes", S, U32)
        z_plane = sb("z_plane", S, U8)
        first_banks = [h2_banks[0], h_banks[0], h_banks[1], h_banks[3]]

        def scale_and_round(c):
            nc.vector.scalar_tensor_tensor(
                out=z_bf[c][:].rearrange("p (n t) -> p n t", t=PACK),
                in0=h_banks[c][:].rearrange("p (t n) -> p n t", t=PACK),
                scalar=0.0625,
                in1=gain[:].unsqueeze(1).to_broadcast([P, CHUNK, PACK]),
                op0=MULT,
                op1=MULT,
            )

        def first_rows(c):
            cols = slice(c * CHUNK, (c + 1) * CHUNK)
            nc.vector.quantize_mx(out=z_codes[:, cols].bitcast(FP8X4), scales=z_plane[:, cols], in_=z_bf[c][:])
            nc.tensor.matmul_mx(
                out=first_banks[c][:, cols],
                lhsT=w_codes0[:].bitcast(FP8X4),
                lhsT_scale=w_plane[:, 0:P],
                rhs=z_codes[:, cols].bitcast(FP8X4),
                rhs_scale=z_plane[:, cols],
                start=True,
                stop=True,
            )
            nc.scalar.copy(rows[0][:, cols], first_banks[c][:, cols])

        gain16 = sb("gain16", PACK, F32)
        nc.scalar.activation(gain16[:], gain[:], COPY, scale=0.0625)
        scale_and_round(0)
        z_flat = sb("z_flat", PACK * CHUNK, BF16)
        for t in range(PACK):
            cols = slice(t * CHUNK, (t + 1) * CHUNK)
            nc.scalar.activation(z_flat[:, cols], h_banks[3][:, cols], COPY, scale=gain16[:, t : t + 1])
        nc.scalar.copy(
            z_bf[3][:].rearrange("p (a b t) -> p a t b", t=PACK, b=4),
            z_flat[:].rearrange("p (t a b) -> p a t b", t=PACK, b=4),
        )
        scale_and_round(1)
        first_rows(0)
        scale_and_round(2)
        for c in (1, 3, 2):
            first_rows(c)
        w_codes = sb("w_codes", N - P, U32, tag="z_bf2")
        w_plane_rest = sb("w_plane_rest", N - P, U8)
        nc.vector.quantize_mx(out=w_codes[:].bitcast(FP8X4), scales=w_plane_rest[:], in_=w_bf[:, PACK * P : PACK * N])

        out_rows = out.rearrange("(p u) j -> u p j", u=PACK)
        for u in range(PACK):
            pa = sb("pa%d" % u, W, F32)
            pb = sb("pb%d" % u, W, F32)
            ra = sb("ra%d" % u, W, F32)
            if u > 0:
                cols = slice((u - 1) * P, u * P)
                nc.tensor.matmul_mx(
                    out=h2_banks[u][:],
                    lhsT=w_codes[:, cols].bitcast(FP8X4),
                    lhsT_scale=w_plane_rest[:, cols],
                    rhs=z_codes[:].bitcast(FP8X4),
                    rhs_scale=z_plane[:],
                    start=True,
                    stop=True,
                )
                nc.scalar.copy(rows[u][:], h2_banks[u][:])
            nc.scalar.activation(pb[:], rows[u][:].indirect(n2_list[:]), COPY)
            if u == 0:
                nc.vector.tensor_copy(pa[:], rows[u][:].indirect(n1_list[:]))
            else:
                nc.scalar.activation(pa[:], rows[u][:].indirect(n1_list[:]), COPY)
            nc.vector.tensor_max(ra[:], pa[:], pb[:])
            nc.vector.tensor_copy(rows[u][:].indirect(n1_list[:]), ra[:])
            nc.sync.dma_start(out_rows[u], rows[u][:])
